import numpy as np
import ml_dtypes


def mxq(x, axis, fmt="e4m3"):
    dtype, down = {"e4m3": (ml_dtypes.float8_e4m3fn, 7), "e5m2": (ml_dtypes.float8_e5m2, 14)}[fmt]
    v = np.moveaxis(np.asarray(x, np.float32).astype(ml_dtypes.bfloat16).astype(np.float64), axis, -1)
    blocks = v.reshape(v.shape[:-1] + (-1, 32))
    amax = np.abs(blocks).max(-1, keepdims=True)
    byte = np.maximum(np.where(amax > 0, np.frexp(amax)[1] - 1 + 127, 0) - down, 1)
    scale = np.exp2(byte - 127.0)
    codes = (blocks / scale).astype(np.float32).astype(dtype).astype(np.float64)
    return np.moveaxis((codes * scale).reshape(v.shape), -1, axis)


WIDE = False


def mx_kscale(k):
    if not WIDE:
        return np.ones(k)
    levels = np.array([10, -10, 5, -5, 0])
    if k % 512:
        return np.exp2(np.random.permutation(np.resize(levels, k // 32))).repeat(32)
    a = np.empty((k // 512, 16))
    for p in range(k // 512):
        a[p, :8] = np.random.permutation(np.resize(levels, 8))
        for g in range(8):
            far = levels[np.abs(levels - a[p, g]) >= 10]
            a[p, g + 8] = far[np.random.randint(len(far))]
    return np.exp2(a.ravel()).repeat(32)


def f64(x):
    return np.asarray(x).astype(np.float64)


def striped8(idx):
    return np.asarray(idx).reshape(8, -1, 16).transpose(0, 2, 1).reshape(128, -1).astype(np.uint16)


def unstriped8(offs):
    return offs.reshape(8, 16, -1).transpose(0, 2, 1).reshape(8, -1).astype(np.int64)


def pick8(x, idx, run):
    r = np.arange(len(x))
    return x[r[:, None], idx[r % (8 * run) // run]]


E2M1 = np.array([0.0, 0.5, 1.0, 1.5, 2.0, 3.0, 4.0, 6.0, -0.0, -0.5, -1.0, -1.5, -2.0, -3.0, -4.0, -6.0])


def pack_weight(w, fmt):
    k, n = w.shape
    w = f64(np.asarray(w, np.float32).astype(ml_dtypes.bfloat16)).reshape(k // 32, 32, n)
    amax = np.abs(w).max(1)
    if fmt == "e4m3":
        byte = np.frexp(amax)[1] - 1 + 127 - 7
    else:
        mant, ex = np.frexp(amax / 6.0)
        byte = np.where(mant > 0.5, ex, ex - 1) + 127
    byte = np.clip(np.where(amax > 0, byte, 1), 1, 254)
    scaled = (w * np.exp2(127.0 - byte)[:, None, :]).reshape(k, n).astype(np.float32)
    by_word = np.ascontiguousarray(scaled.reshape(k // 512, 128, 4, n).transpose(0, 1, 3, 2))
    if fmt == "e4m3":
        words = by_word.astype(ml_dtypes.float8_e4m3fn).view(np.uint8)
    else:
        c = by_word.astype(ml_dtypes.float4_e2m1fn).view(np.uint8) & 0xF
        words = (c[..., 0::2] | (c[..., 1::2] << 4)).reshape(k // 512, 128, 2 * n)
    return np.ascontiguousarray(words), np.ascontiguousarray(byte.astype(np.uint8).reshape(k // 512, 16, n))


def unpack_weight(words, scales, fmt):
    g, _, n = scales.shape
    words = np.ascontiguousarray(words).reshape(g, 128, n, -1)
    if fmt == "e4m3":
        vals = words.view(ml_dtypes.float8_e4m3fn).astype(np.float64)
    else:
        nib = np.empty((g, 128, n, 4), np.uint8)
        nib[..., 0::2] = words & 0xF
        nib[..., 1::2] = words >> 4
        vals = E2M1[nib]
    vals = vals * np.repeat(np.exp2(scales.astype(np.float64) - 127.0), 8, axis=1)[..., None]
    return vals.transpose(0, 1, 3, 2).reshape(g * 512, n)


def sigmoid(v):
    return 1.0 / (1.0 + np.exp(-v))


D, V, Q, I = 512, 2048, 128, 512


def setup_inputs():
    n = np.random.standard_normal
    idx = np.stack([np.random.permutation(V)[:I] for _ in range(8)])
    idx2 = np.stack([np.random.permutation(V)[:I] for _ in range(8)])
    fd = mx_kscale(D)
    vocp = pack_weight(n((D, V)) / fd[:, None], "e2m1")
    return {
        "hid": (n((D, Q)) * 1.0 / np.sqrt(D) * fd[:, None]).astype(np.float32),
        "voc_words": vocp[0],
        "voc_scales": vocp[1],
        "margin": (np.random.uniform(0.0, 1.0, (1, I))).astype(np.float32),
        "steep": (np.random.uniform(1.0, 3.0, (Q, 1))).astype(np.float32),
        "dhid": (n((D, Q)) * 1.0 / np.sqrt(D) * fd[:, None]).astype(np.float32),
        "base": (0.5 * n((Q, V))).astype(np.float32),
        "offs": striped8(idx),
        "offs2": striped8(idx2),
    }


def reference(hid, voc_words, voc_scales, margin, steep, dhid, base, offs, offs2):
    idx = unstriped8(offs)
    idx2 = unstriped8(offs2)
    vocu = unpack_weight(voc_words, voc_scales, "e2m1")
    hidq = mxq(f64(hid), 0, "e4m3")
    a = hidq.T @ vocu
    dhidq = mxq(f64(dhid), 0, "e4m3")
    ta = dhidq.T @ vocu
    b = pick8(a, idx2, 16) - pick8(a, idx, 16)
    xb = pick8(ta, idx2, 16) - pick8(ta, idx, 16)
    xdb = xb * f64(steep) * sigmoid((b + f64(margin)) * f64(steep)) * (1.0 - sigmoid((b + f64(margin)) * f64(steep))) * f64(steep)
    xs1 = np.zeros((Q, V))
    xs1[np.arange(Q)[:, None], idx2[np.arange(Q) % 128 // 16]] = xdb
    xe2 = xdb * (-1.0)
    xs2 = np.zeros((Q, V))
    xs2[np.arange(Q)[:, None], idx[np.arange(Q) % 128 // 16]] = xe2
    xda = xs1 + xs2
    y = xda + f64(base)
    return y

@@ -1,0 +1,181 @@
+from contextlib import ExitStack
+
+import concourse.mybir as mybir
+from concourse.masks import make_identity
+
+D, V, Q, I = 512, 2048, 128, 512
+FLOPS = 2 * 2 * D * Q * V
+
+F32 = mybir.dt.float32
+BF16 = mybir.dt.bfloat16
+I32 = mybir.dt.int32
+U32 = mybir.dt.uint32
+U16 = mybir.dt.uint16
+U8 = mybir.dt.uint8
+FP8X4 = mybir.dt.float8_e4m3fn_x4
+FP4X4 = mybir.dt.float4_e2m1fn_x4
+ALU = mybir.AluOpType
+ACT = mybir.ActivationFunctionType
+
+P = 128
+PACK = 4
+BANK = 512
+WORD_LOADS = 2
+A_WIDTHS = (512, 512, 512, 256, 256)
+TA_WIDTHS = (512, 512, 512, 512)
+STORE_WIDTHS = (256, 256, 512, 512, 256, 256)
+
+
+def spans(widths):
+    starts = [sum(widths[:k]) for k in range(len(widths))]
+    return [slice(s, s + w) for s, w in zip(starts, widths)]
+
+
+def tile_attend_hvpairmargin_heads_kernel(tc, hid, voc_words, voc_scales, margin, steep, dhid, base, offs, offs2, out):
+    nc = tc.nc
+    with ExitStack() as ctx:
+        keep = ctx.enter_context(tc.tile_pool(name="keep", bufs=1))
+        psum = ctx.enter_context(tc.psum_pool(name="psum", bufs=8))
+
+        def bank():
+            return psum.tile([P, BANK], F32, name="bank")
+
+        scales = keep.tile([P, V], U8, name="scales", align_bytes=64)
+        nc.vector.memset(scales[:].bitcast(U32), 0)
+        zero = keep.tile([P, 1], F32, name="zero")
+        nc.gpsimd.memset(zero[:], 0.0)
+        half = keep.tile([P, 1], F32, name="half")
+        nc.scalar.activation(half[:], zero[:], ACT.Sigmoid)
+        ident = keep.tile([P, P], F32, name="ident")
+        make_identity(nc, ident[:])
+
+        hid_raw = keep.tile([P, PACK, Q], F32, name="hid_raw")
+        nc.sync.dma_start(hid_raw[:], hid.rearrange("(p j) q -> p j q", j=PACK))
+        margin_col = keep.tile([P, PACK], F32, name="margin_col")
+        nc.sync.dma_start(margin_col[:], margin.rearrange("o (p j) -> (o p) j", j=PACK))
+        for quad in range(4):
+            nc.sync.dma_start(
+                scales[32 * quad : 32 * quad + 4, :].bitcast(I32),
+                voc_scales[0, 4 * quad : 4 * quad + 4, :].bitcast(I32),
+            )
+        word_cols = V // WORD_LOADS
+        words = []
+        for k in range(WORD_LOADS):
+            w = keep.tile([P, 2 * word_cols], U8, name=f"words{k}", align_bytes=64)
+            nc.sync.dma_start(w[:].bitcast(I32), voc_words[0, :, 2 * word_cols * k : 2 * word_cols * (k + 1)].bitcast(I32))
+            words.append(w)
+        dhid_raw = keep.tile([P, PACK, Q], F32, name="dhid_raw")
+        nc.sync.dma_start(dhid_raw[:], dhid.rearrange("(p j) q -> p j q", j=PACK))
+        lists = keep.tile([P, I // 16], U16, name="lists")
+        nc.sync.dma_start(lists[:], offs)
+        lists2 = keep.tile([P, I // 16], U16, name="lists2")
+        nc.sync.dma_start(lists2[:], offs2)
+        steep_col = keep.tile([P, 1], F32, name="steep_col")
+        nc.sync.dma_start(steep_col[:], steep)
+        base_sb = keep.tile([P, V], F32, name="base_sb")
+        nc.sync.dma_start(base_sb[:], base)
+
+        xs1 = keep.tile([P, V], F32, name="xs1")
+        nc.vector.memset(xs1[:], 0.0)
+
+        margin_ps = bank()
+        for j in range(PACK):
+            nc.tensor.transpose(margin_ps[:, j * P : (j + 1) * P], margin_col[:, j : j + 1].to_broadcast([P, P]), ident[:])
+        margin_all = keep.tile([P, P, PACK], F32, name="margin_all")
+        nc.scalar.copy(margin_all[:], margin_ps[:].rearrange("q (j p) -> q p j", j=PACK))
+
+        def quantise(raw, name, tag):
+            grouped = keep.tile([P, Q * PACK], BF16, name=name + "_bf", tag=tag, align_bytes=64)
+            nc.vector.tensor_copy(
+                grouped[:].rearrange("p (c i t) -> p c t i", i=4, t=PACK),
+                raw[:].rearrange("p t (c i) -> p c t i", i=4),
+            )
+            codes = keep.tile([P, Q], U32, name=name + "_codes", align_bytes=64)
+            plane = keep.tile([P, Q], U8, name=name + "_plane", align_bytes=64)
+            nc.vector.quantize_mx(out=codes[:].bitcast(FP8X4), scales=plane[:], in_=grouped[:])
+            return codes, plane
+
+        def scores(codes, plane, widths, dest, copy_engines):
+            for cols, eng in zip(spans(widths), copy_engines):
+                acc = bank()
+                n = cols.stop - cols.start
+                k, c0 = divmod(cols.start, word_cols)
+                nc.tensor.matmul_mx(
+                    out=acc[:, :n],
+                    lhsT=codes[:].bitcast(FP8X4),
+                    lhsT_scale=plane[:],
+                    rhs=words[k][:, 2 * c0 : 2 * (c0 + n)].bitcast(FP4X4),
+                    rhs_scale=scales[:, cols],
+                    start=True,
+                    stop=True,
+                )
+                eng(dest[:, cols], acc[:, :n])
+
+        s_copy, v_copy = nc.scalar.copy, nc.vector.tensor_copy
+        hq = quantise(hid_raw, "hid", "late_window")
+        a_sb = keep.tile([P, V], F32, name="a_sb")
+        scores(*hq, A_WIDTHS, a_sb, (s_copy, s_copy, s_copy, v_copy, s_copy))
+        xs2 = keep.tile([P, V], F32, name="xs2", tag="late_window", align_bytes=64)
+        nc.vector.memset(xs2[:], 0.0)
+        dq = quantise(dhid_raw, "dhid", "dhid_bf")
+        ta_sb = keep.tile([P, V], F32, name="ta_sb")
+        scores(*dq, TA_WIDTHS, ta_sb, (s_copy,) * 4)
+
+        c_pos = keep.tile([P, 1], F32, name="c_pos")
+        c_neg = keep.tile([P, 1], F32, name="c_neg")
+        q_pos = keep.tile([P, 1], F32, name="q_pos")
+        q_neg = keep.tile([P, 1], F32, name="q_neg")
+        nc.gpsimd.tensor_tensor(c_pos[:], steep_col[:], steep_col[:], ALU.mult)
+        nc.gpsimd.tensor_scalar(c_neg[:], c_pos[:], -1.0, 0.0, ALU.mult, ALU.add)
+        nc.gpsimd.tensor_scalar(q_pos[:], c_pos[:], 0.25, 0.0, ALU.mult, ALU.add)
+        nc.gpsimd.tensor_scalar(q_neg[:], c_pos[:], -0.25, 0.0, ALU.mult, ALU.add)
+
+        first = keep.tile([P, I], F32, name="first")
+        nc.vector.tensor_tensor(first[:], a_sb[:].indirect(lists[:]), margin_all[:].rearrange("q p j -> q (p j)"), ALU.subtract)
+        z = keep.tile([P, I], F32, name="z")
+        nc.vector.tensor_tensor(z[:], a_sb[:].indirect(lists2[:]), first[:], ALU.subtract)
+        tfirst = keep.tile([P, I], F32, name="tfirst")
+        nc.vector.tensor_copy(tfirst[:], ta_sb[:].indirect(lists[:]))
+        xb = keep.tile([P, I], F32, name="xb")
+        nc.vector.tensor_tensor(xb[:], ta_sb[:].indirect(lists2[:]), tfirst[:], ALU.subtract)
+
+        sig = keep.tile([P, I], F32, name="sig")
+        nc.scalar.activation(sig[:], z[:], ACT.Sigmoid, scale=steep_col[:])
+        sq = keep.tile([P, I], F32, name="sq")
+        nc.scalar.activation(sq[:], sig[:], ACT.Square, bias=half[:], scale=-1.0)
+        w_pos = keep.tile([P, I], F32, name="w_pos")
+        nc.scalar.activation(w_pos[:], sq[:], ACT.Identity, bias=q_pos[:], scale=c_neg[:])
+        w_neg = keep.tile([P, I], F32, name="w_neg")
+        nc.scalar.activation(w_neg[:], sq[:], ACT.Identity, bias=q_neg[:], scale=c_pos[:])
+
+        nc.vector.tensor_tensor(xs1[:].indirect(lists2[:]), xb[:], w_pos[:], ALU.mult)
+        nc.vector.tensor_tensor(xs2[:].indirect(lists[:]), xb[:], w_neg[:], ALU.mult)
+
+        blocks = BANK // P
+        turned = []
+        for g in range(V // BANK):
+            acc = bank()
+            for src, first_src, last_src in ((base_sb, True, False), (xs1, False, True)):
+                for j in range(blocks):
+                    c = g * BANK + j * P
+                    nc.tensor.matmul(
+                        acc[:, j * P : (j + 1) * P], src[:, c : c + P], ident[:],
+                        start=(first_src and j == 0), stop=(last_src and j == blocks - 1), is_transpose=True,
+                    )
+            t_sb = keep.tile([P, BANK], F32, name=f"turned{g}")
+            nc.scalar.copy(t_sb[:], acc[:])
+            turned.append(t_sb)
+        partial = []
+        for g in range(V // BANK):
+            acc = bank()
+            for j in range(blocks):
+                nc.tensor.transpose(acc[:, j * P : (j + 1) * P], turned[g][:, j * P : (j + 1) * P], ident[:])
+            partial.append(acc)
+
+        for k, cols in enumerate(spans(STORE_WIDTHS)):
+            g, c0 = divmod(cols.start, BANK)
+            n = cols.stop - cols.start
+            res = keep.tile([P, n], F32, name=f"res{k}")
+            nc.vector.tensor_tensor(res[:], partial[g][:, c0 : c0 + n], xs2[:, cols], ALU.add)
+            queue = nc.sync if k % 2 == 0 else nc.scalar
+            queue.dma_start(out[:, cols], res[:])

@@ -23,7 +23,7 @@ BANK = 512
 WORD_LOADS = 2
 A_WIDTHS = (512, 512, 512, 256, 256)
 TA_WIDTHS = (512, 512, 512, 512)
-STORE_WIDTHS = (256, 256, 512, 512, 256, 256)
+STORE_WIDTHS = (128, 384, 512, 512, 256, 256)
 
 
 def spans(widths):
@@ -48,16 +48,15 @@ def tile_attend_hvpairmargin_heads_kernel(tc, hid, voc_words, voc_scales, margin
         nc.scalar.activation(half[:], zero[:], ACT.Sigmoid)
         ident = keep.tile([P, P], F32, name="ident")
         make_identity(nc, ident[:])
+        steep_col = keep.tile([P, 1], F32, name="steep_col")
+        nc.gpsimd.dma_start(steep_col[:], steep)
 
         hid_raw = keep.tile([P, PACK, Q], F32, name="hid_raw")
         nc.sync.dma_start(hid_raw[:], hid.rearrange("(p j) q -> p j q", j=PACK))
         margin_col = keep.tile([P, PACK], F32, name="margin_col")
         nc.sync.dma_start(margin_col[:], margin.rearrange("o (p j) -> (o p) j", j=PACK))
-        for quad in range(4):
-            nc.sync.dma_start(
-                scales[32 * quad : 32 * quad + 4, :].bitcast(I32),
-                voc_scales[0, 4 * quad : 4 * quad + 4, :].bitcast(I32),
-            )
+        for r in range(4):
+            nc.sync.dma_start(scales[r:P:32, :].bitcast(I32), voc_scales[0, r:16:4, :].bitcast(I32))
         word_cols = V // WORD_LOADS
         words = []
         for k in range(WORD_LOADS):
@@ -70,8 +69,6 @@ def tile_attend_hvpairmargin_heads_kernel(tc, hid, voc_words, voc_scales, margin
         nc.sync.dma_start(lists[:], offs)
         lists2 = keep.tile([P, I // 16], U16, name="lists2")
         nc.sync.dma_start(lists2[:], offs2)
-        steep_col = keep.tile([P, 1], F32, name="steep_col")
-        nc.sync.dma_start(steep_col[:], steep)
         base_sb = keep.tile([P, V], F32, name="base_sb")
         nc.sync.dma_start(base_sb[:], base)
 
@@ -112,41 +109,42 @@ def tile_attend_hvpairmargin_heads_kernel(tc, hid, voc_words, voc_scales, margin
                 eng(dest[:, cols], acc[:, :n])
 
         s_copy, v_copy = nc.scalar.copy, nc.vector.tensor_copy
-        hq = quantise(hid_raw, "hid", "late_window")
-        a_sb = keep.tile([P, V], F32, name="a_sb")
-        scores(*hq, A_WIDTHS, a_sb, (s_copy, s_copy, s_copy, v_copy, s_copy))
-        xs2 = keep.tile([P, V], F32, name="xs2", tag="late_window", align_bytes=64)
-        nc.vector.memset(xs2[:], 0.0)
+        hq = quantise(hid_raw, "hid", "hid_bf")
         dq = quantise(dhid_raw, "dhid", "dhid_bf")
+        a_sb = keep.tile([P, V], F32, name="a_sb")
+        scores(*hq, A_WIDTHS, a_sb, (s_copy, s_copy, v_copy, s_copy, s_copy))
         ta_sb = keep.tile([P, V], F32, name="ta_sb")
         scores(*dq, TA_WIDTHS, ta_sb, (s_copy,) * 4)
 
-        c_pos = keep.tile([P, 1], F32, name="c_pos")
         c_neg = keep.tile([P, 1], F32, name="c_neg")
         q_pos = keep.tile([P, 1], F32, name="q_pos")
-        q_neg = keep.tile([P, 1], F32, name="q_neg")
-        nc.gpsimd.tensor_tensor(c_pos[:], steep_col[:], steep_col[:], ALU.mult)
-        nc.gpsimd.tensor_scalar(c_neg[:], c_pos[:], -1.0, 0.0, ALU.mult, ALU.add)
-        nc.gpsimd.tensor_scalar(q_pos[:], c_pos[:], 0.25, 0.0, ALU.mult, ALU.add)
-        nc.gpsimd.tensor_scalar(q_neg[:], c_pos[:], -0.25, 0.0, ALU.mult, ALU.add)
+        nc.scalar.activation(q_pos[:], steep_col[:], ACT.Square, scale=0.5)
+        nc.scalar.activation(c_neg[:], q_pos[:], ACT.Copy, scale=-4.0)
 
         first = keep.tile([P, I], F32, name="first")
         nc.vector.tensor_tensor(first[:], a_sb[:].indirect(lists[:]), margin_all[:].rearrange("q p j -> q (p j)"), ALU.subtract)
         z = keep.tile([P, I], F32, name="z")
         nc.vector.tensor_tensor(z[:], a_sb[:].indirect(lists2[:]), first[:], ALU.subtract)
-        tfirst = keep.tile([P, I], F32, name="tfirst")
+        tfirst = keep.tile([P, I], F32, name="tfirst", tag="late_window")
         nc.vector.tensor_copy(tfirst[:], ta_sb[:].indirect(lists[:]))
         xb = keep.tile([P, I], F32, name="xb")
         nc.vector.tensor_tensor(xb[:], ta_sb[:].indirect(lists2[:]), tfirst[:], ALU.subtract)
+        xs2 = keep.tile([P, V], F32, name="xs2", tag="late_window")
+        nc.gpsimd.memset(xs2[:], 0.0)
 
+
+        halves = spans((I // 2, I // 2))
         sig = keep.tile([P, I], F32, name="sig")
-        nc.scalar.activation(sig[:], z[:], ACT.Sigmoid, scale=steep_col[:])
         sq = keep.tile([P, I], F32, name="sq")
-        nc.scalar.activation(sq[:], sig[:], ACT.Square, bias=half[:], scale=-1.0)
         w_pos = keep.tile([P, I], F32, name="w_pos")
-        nc.scalar.activation(w_pos[:], sq[:], ACT.Identity, bias=q_pos[:], scale=c_neg[:])
+        for h in halves:
+            nc.scalar.activation(sig[:, h], z[:, h], ACT.Sigmoid, scale=steep_col[:])
+        for h in halves:
+            nc.scalar.activation(sq[:, h], sig[:, h], ACT.Square, bias=half[:], scale=-1.0)
+        for h in halves:
+            nc.scalar.activation(w_pos[:, h], sq[:, h], ACT.Identity, bias=q_pos[:], scale=c_neg[:])
         w_neg = keep.tile([P, I], F32, name="w_neg")
-        nc.scalar.activation(w_neg[:], sq[:], ACT.Identity, bias=q_neg[:], scale=c_pos[:])
+        nc.scalar.activation(w_neg[:], w_pos[:], ACT.Copy, scale=-1.0)
 
         nc.vector.tensor_tensor(xs1[:].indirect(lists2[:]), xb[:], w_pos[:], ALU.mult)
         nc.vector.tensor_tensor(xs2[:].indirect(lists[:]), xb[:], w_neg[:], ALU.mult)

@@ -48,8 +48,6 @@ def tile_attend_hvpairmargin_heads_kernel(tc, hid, voc_words, voc_scales, margin
         nc.scalar.activation(half[:], zero[:], ACT.Sigmoid)
         ident = keep.tile([P, P], F32, name="ident")
         make_identity(nc, ident[:])
-        steep_col = keep.tile([P, 1], F32, name="steep_col")
-        nc.gpsimd.dma_start(steep_col[:], steep)
 
         hid_raw = keep.tile([P, PACK, Q], F32, name="hid_raw")
         nc.sync.dma_start(hid_raw[:], hid.rearrange("(p j) q -> p j q", j=PACK))
@@ -69,6 +67,8 @@ def tile_attend_hvpairmargin_heads_kernel(tc, hid, voc_words, voc_scales, margin
         nc.sync.dma_start(lists[:], offs)
         lists2 = keep.tile([P, I // 16], U16, name="lists2")
         nc.sync.dma_start(lists2[:], offs2)
+        steep_col = keep.tile([P, 1], F32, name="steep_col")
+        nc.sync.dma_start(steep_col[:], steep)
         base_sb = keep.tile([P, V], F32, name="base_sb")
         nc.sync.dma_start(base_sb[:], base)
 
@@ -81,12 +81,13 @@ def tile_attend_hvpairmargin_heads_kernel(tc, hid, voc_words, voc_scales, margin
         margin_all = keep.tile([P, P, PACK], F32, name="margin_all")
         nc.scalar.copy(margin_all[:], margin_ps[:].rearrange("q (j p) -> q p j", j=PACK))
 
-        def quantise(raw, name, tag):
+        def quantise(raw, name, tag, on_vector):
             grouped = keep.tile([P, Q * PACK], BF16, name=name + "_bf", tag=tag, align_bytes=64)
-            nc.vector.tensor_copy(
-                grouped[:].rearrange("p (c i t) -> p c t i", i=4, t=PACK),
-                raw[:].rearrange("p t (c i) -> p c t i", i=4),
-            )
+            dst = grouped[:].rearrange("p (c i t) -> p c t i", i=4, t=PACK)
+            src = raw[:].rearrange("p t (c i) -> p c t i", i=4)
+            nc.vector.tensor_copy(dst[:, :on_vector], src[:, :on_vector])
+            if on_vector < Q // 4:
+                nc.scalar.copy(dst[:, on_vector:], src[:, on_vector:])
             codes = keep.tile([P, Q], U32, name=name + "_codes", align_bytes=64)
             plane = keep.tile([P, Q], U8, name=name + "_plane", align_bytes=64)
             nc.vector.quantize_mx(out=codes[:].bitcast(FP8X4), scales=plane[:], in_=grouped[:])
@@ -109,8 +110,10 @@ def tile_attend_hvpairmargin_heads_kernel(tc, hid, voc_words, voc_scales, margin
                 eng(dest[:, cols], acc[:, :n])
 
         s_copy, v_copy = nc.scalar.copy, nc.vector.tensor_copy
-        hq = quantise(hid_raw, "hid", "hid_bf")
-        dq = quantise(dhid_raw, "dhid", "dhid_bf")
+        hq = quantise(hid_raw, "hid", "late_window", 20)
+        xs2 = keep.tile([P, V], F32, name="xs2", tag="late_window", align_bytes=64)
+        nc.vector.memset(xs2[:], 0.0)
+        dq = quantise(dhid_raw, "dhid", "dhid_bf", 32)
         a_sb = keep.tile([P, V], F32, name="a_sb")
         scores(*hq, A_WIDTHS, a_sb, (s_copy, s_copy, v_copy, s_copy, s_copy))
         ta_sb = keep.tile([P, V], F32, name="ta_sb")
@@ -118,19 +121,19 @@ def tile_attend_hvpairmargin_heads_kernel(tc, hid, voc_words, voc_scales, margin
 
         c_neg = keep.tile([P, 1], F32, name="c_neg")
         q_pos = keep.tile([P, 1], F32, name="q_pos")
-        nc.scalar.activation(q_pos[:], steep_col[:], ACT.Square, scale=0.5)
-        nc.scalar.activation(c_neg[:], q_pos[:], ACT.Copy, scale=-4.0)
+        c_pos = keep.tile([P, 1], F32, name="c_pos")
+        nc.gpsimd.tensor_tensor(c_pos[:], steep_col[:], steep_col[:], ALU.mult)
+        nc.gpsimd.tensor_scalar(c_neg[:], c_pos[:], -1.0, 0.0, ALU.mult, ALU.add)
+        nc.gpsimd.tensor_scalar(q_pos[:], c_pos[:], 0.25, 0.0, ALU.mult, ALU.add)
 
         first = keep.tile([P, I], F32, name="first")
         nc.vector.tensor_tensor(first[:], a_sb[:].indirect(lists[:]), margin_all[:].rearrange("q p j -> q (p j)"), ALU.subtract)
         z = keep.tile([P, I], F32, name="z")
         nc.vector.tensor_tensor(z[:], a_sb[:].indirect(lists2[:]), first[:], ALU.subtract)
-        tfirst = keep.tile([P, I], F32, name="tfirst", tag="late_window")
+        tfirst = keep.tile([P, I], F32, name="tfirst")
         nc.vector.tensor_copy(tfirst[:], ta_sb[:].indirect(lists[:]))
         xb = keep.tile([P, I], F32, name="xb")
         nc.vector.tensor_tensor(xb[:], ta_sb[:].indirect(lists2[:]), tfirst[:], ALU.subtract)
-        xs2 = keep.tile([P, V], F32, name="xs2", tag="late_window")
-        nc.gpsimd.memset(xs2[:], 0.0)
 
 
         halves = spans((I // 2, I // 2))

from contextlib import ExitStack

import concourse.mybir as mybir
from concourse.masks import make_identity

D, V, Q, I = 512, 2048, 128, 512
FLOPS = 2 * 2 * D * Q * V

F32 = mybir.dt.float32
BF16 = mybir.dt.bfloat16
I32 = mybir.dt.int32
U32 = mybir.dt.uint32
U16 = mybir.dt.uint16
U8 = mybir.dt.uint8
FP8X4 = mybir.dt.float8_e4m3fn_x4
FP4X4 = mybir.dt.float4_e2m1fn_x4
ALU = mybir.AluOpType
ACT = mybir.ActivationFunctionType

P = 128
PACK = 4
BANK = 512
WORD_LOADS = 2
A_WIDTHS = (512, 512, 512, 256, 256)
TA_WIDTHS = (512, 512, 512, 512)
STORE_WIDTHS = (128, 384, 512, 512, 256, 256)


def spans(widths):
    starts = [sum(widths[:k]) for k in range(len(widths))]
    return [slice(s, s + w) for s, w in zip(starts, widths)]


def tile_attend_hvpairmargin_heads_kernel(tc, hid, voc_words, voc_scales, margin, steep, dhid, base, offs, offs2, out):
    nc = tc.nc
    with ExitStack() as ctx:
        keep = ctx.enter_context(tc.tile_pool(name="keep", bufs=1))
        psum = ctx.enter_context(tc.psum_pool(name="psum", bufs=8))

        def bank():
            return psum.tile([P, BANK], F32, name="bank")

        scales = keep.tile([P, V], U8, name="scales", align_bytes=64)
        nc.vector.memset(scales[:].bitcast(U32), 0)
        zero = keep.tile([P, 1], F32, name="zero")
        nc.gpsimd.memset(zero[:], 0.0)
        half = keep.tile([P, 1], F32, name="half")
        nc.scalar.activation(half[:], zero[:], ACT.Sigmoid)
        ident = keep.tile([P, P], F32, name="ident")
        make_identity(nc, ident[:])

        hid_raw = keep.tile([P, PACK, Q], F32, name="hid_raw")
        nc.sync.dma_start(hid_raw[:], hid.rearrange("(p j) q -> p j q", j=PACK))
        margin_col = keep.tile([P, PACK], F32, name="margin_col")
        nc.sync.dma_start(margin_col[:], margin.rearrange("o (p j) -> (o p) j", j=PACK))
        for r in range(4):
            nc.sync.dma_start(scales[r:P:32, :].bitcast(I32), voc_scales[0, r:16:4, :].bitcast(I32))
        word_cols = V // WORD_LOADS
        words = []
        for k in range(WORD_LOADS):
            w = keep.tile([P, 2 * word_cols], U8, name=f"words{k}", align_bytes=64)
            nc.sync.dma_start(w[:].bitcast(I32), voc_words[0, :, 2 * word_cols * k : 2 * word_cols * (k + 1)].bitcast(I32))
            words.append(w)
        dhid_raw = keep.tile([P, PACK, Q], F32, name="dhid_raw")
        nc.sync.dma_start(dhid_raw[:], dhid.rearrange("(p j) q -> p j q", j=PACK))
        lists = keep.tile([P, I // 16], U16, name="lists")
        nc.sync.dma_start(lists[:], offs)
        lists2 = keep.tile([P, I // 16], U16, name="lists2")
        nc.sync.dma_start(lists2[:], offs2)
        steep_col = keep.tile([P, 1], F32, name="steep_col")
        nc.sync.dma_start(steep_col[:], steep)
        base_sb = keep.tile([P, V], F32, name="base_sb")
        nc.sync.dma_start(base_sb[:], base)

        xs1 = keep.tile([P, V], F32, name="xs1")
        nc.vector.memset(xs1[:], 0.0)

        margin_ps = bank()
        for j in range(PACK):
            nc.tensor.transpose(margin_ps[:, j * P : (j + 1) * P], margin_col[:, j : j + 1].to_broadcast([P, P]), ident[:])
        margin_all = keep.tile([P, P, PACK], F32, name="margin_all")
        nc.scalar.copy(margin_all[:], margin_ps[:].rearrange("q (j p) -> q p j", j=PACK))

        def quantise(raw, name, tag, on_vector):
            grouped = keep.tile([P, Q * PACK], BF16, name=name + "_bf", tag=tag, align_bytes=64)
            dst = grouped[:].rearrange("p (c i t) -> p c t i", i=4, t=PACK)
            src = raw[:].rearrange("p t (c i) -> p c t i", i=4)
            nc.vector.tensor_copy(dst[:, :on_vector], src[:, :on_vector])
            if on_vector < Q // 4:
                nc.scalar.copy(dst[:, on_vector:], src[:, on_vector:])
            codes = keep.tile([P, Q], U32, name=name + "_codes", align_bytes=64)
            plane = keep.tile([P, Q], U8, name=name + "_plane", align_bytes=64)
            nc.vector.quantize_mx(out=codes[:].bitcast(FP8X4), scales=plane[:], in_=grouped[:])
            return codes, plane

        def scores(codes, plane, widths, dest, copy_engines):
            for cols, eng in zip(spans(widths), copy_engines):
                acc = bank()
                n = cols.stop - cols.start
                k, c0 = divmod(cols.start, word_cols)
                nc.tensor.matmul_mx(
                    out=acc[:, :n],
                    lhsT=codes[:].bitcast(FP8X4),
                    lhsT_scale=plane[:],
                    rhs=words[k][:, 2 * c0 : 2 * (c0 + n)].bitcast(FP4X4),
                    rhs_scale=scales[:, cols],
                    start=True,
                    stop=True,
                )
                eng(dest[:, cols], acc[:, :n])

        s_copy, v_copy = nc.scalar.copy, nc.vector.tensor_copy
        hq = quantise(hid_raw, "hid", "late_window", 20)
        xs2 = keep.tile([P, V], F32, name="xs2", tag="late_window", align_bytes=64)
        nc.vector.memset(xs2[:], 0.0)
        dq = quantise(dhid_raw, "dhid", "dhid_bf", 32)
        a_sb = keep.tile([P, V], F32, name="a_sb")
        scores(*hq, A_WIDTHS, a_sb, (s_copy, s_copy, v_copy, s_copy, s_copy))
        ta_sb = keep.tile([P, V], F32, name="ta_sb")
        scores(*dq, TA_WIDTHS, ta_sb, (s_copy,) * 4)

        c_neg = keep.tile([P, 1], F32, name="c_neg")
        q_pos = keep.tile([P, 1], F32, name="q_pos")
        c_pos = keep.tile([P, 1], F32, name="c_pos")
        nc.gpsimd.tensor_tensor(c_pos[:], steep_col[:], steep_col[:], ALU.mult)
        nc.gpsimd.tensor_scalar(c_neg[:], c_pos[:], -1.0, 0.0, ALU.mult, ALU.add)
        nc.gpsimd.tensor_scalar(q_pos[:], c_pos[:], 0.25, 0.0, ALU.mult, ALU.add)

        first = keep.tile([P, I], F32, name="first")
        nc.vector.tensor_tensor(first[:], a_sb[:].indirect(lists[:]), margin_all[:].rearrange("q p j -> q (p j)"), ALU.subtract)
        z = keep.tile([P, I], F32, name="z")
        nc.vector.tensor_tensor(z[:], a_sb[:].indirect(lists2[:]), first[:], ALU.subtract)
        tfirst = keep.tile([P, I], F32, name="tfirst")
        nc.vector.tensor_copy(tfirst[:], ta_sb[:].indirect(lists[:]))
        xb = keep.tile([P, I], F32, name="xb")
        nc.vector.tensor_tensor(xb[:], ta_sb[:].indirect(lists2[:]), tfirst[:], ALU.subtract)


        halves = spans((I // 2, I // 2))
        sig = keep.tile([P, I], F32, name="sig")
        sq = keep.tile([P, I], F32, name="sq")
        w_pos = keep.tile([P, I], F32, name="w_pos")
        for h in halves:
            nc.scalar.activation(sig[:, h], z[:, h], ACT.Sigmoid, scale=steep_col[:])
        for h in halves:
            nc.scalar.activation(sq[:, h], sig[:, h], ACT.Square, bias=half[:], scale=-1.0)
        for h in halves:
            nc.scalar.activation(w_pos[:, h], sq[:, h], ACT.Identity, bias=q_pos[:], scale=c_neg[:])
        w_neg = keep.tile([P, I], F32, name="w_neg")
        nc.scalar.activation(w_neg[:], w_pos[:], ACT.Copy, scale=-1.0)

        nc.vector.tensor_tensor(xs1[:].indirect(lists2[:]), xb[:], w_pos[:], ALU.mult)
        nc.vector.tensor_tensor(xs2[:].indirect(lists[:]), xb[:], w_neg[:], ALU.mult)

        blocks = BANK // P
        turned = []
        for g in range(V // BANK):
            acc = bank()
            for src, first_src, last_src in ((base_sb, True, False), (xs1, False, True)):
                for j in range(blocks):
                    c = g * BANK + j * P
                    nc.tensor.matmul(
                        acc[:, j * P : (j + 1) * P], src[:, c : c + P], ident[:],
                        start=(first_src and j == 0), stop=(last_src and j == blocks - 1), is_transpose=True,
                    )
            t_sb = keep.tile([P, BANK], F32, name=f"turned{g}")
            nc.scalar.copy(t_sb[:], acc[:])
            turned.append(t_sb)
        partial = []
        for g in range(V // BANK):
            acc = bank()
            for j in range(blocks):
                nc.tensor.transpose(acc[:, j * P : (j + 1) * P], turned[g][:, j * P : (j + 1) * P], ident[:])
            partial.append(acc)

        for k, cols in enumerate(spans(STORE_WIDTHS)):
            g, c0 = divmod(cols.start, BANK)
            n = cols.stop - cols.start
            res = keep.tile([P, n], F32, name=f"res{k}")
            nc.vector.tensor_tensor(res[:], partial[g][:, c0 : c0 + n], xs2[:, cols], ALU.add)
            queue = nc.sync if k % 2 == 0 else nc.scalar
            queue.dma_start(out[:, cols], res[:])
